import numpy as np
import ml_dtypes


def mxq(x, axis, fmt="e4m3"):
    dtype, down = {"e4m3": (ml_dtypes.float8_e4m3fn, 7), "e5m2": (ml_dtypes.float8_e5m2, 14)}[fmt]
    v = np.moveaxis(np.asarray(x, np.float32).astype(ml_dtypes.bfloat16).astype(np.float64), axis, -1)
    blocks = v.reshape(v.shape[:-1] + (-1, 32))
    amax = np.abs(blocks).max(-1, keepdims=True)
    byte = np.maximum(np.where(amax > 0, np.frexp(amax)[1] - 1 + 127, 0) - down, 1)
    scale = np.exp2(byte - 127.0)
    codes = (blocks / scale).astype(np.float32).astype(dtype).astype(np.float64)
    return np.moveaxis((codes * scale).reshape(v.shape), -1, axis)


WIDE = False


def mx_kscale(k):
    if not WIDE:
        return np.ones(k)
    levels = np.array([10, -10, 5, -5, 0])
    if k % 512:
        return np.exp2(np.random.permutation(np.resize(levels, k // 32))).repeat(32)
    a = np.empty((k // 512, 16))
    for p in range(k // 512):
        a[p, :8] = np.random.permutation(np.resize(levels, 8))
        for g in range(8):
            far = levels[np.abs(levels - a[p, g]) >= 10]
            a[p, g + 8] = far[np.random.randint(len(far))]
    return np.exp2(a.ravel()).repeat(32)


def f64(x):
    return np.asarray(x).astype(np.float64)


def striped8(idx):
    return np.asarray(idx).reshape(8, -1, 16).transpose(0, 2, 1).reshape(128, -1).astype(np.uint16)


def unstriped8(offs):
    return offs.reshape(8, 16, -1).transpose(0, 2, 1).reshape(8, -1).astype(np.int64)


def pick8(x, idx, run):
    r = np.arange(len(x))
    return x[r[:, None], idx[r % (8 * run) // run]]


E2M1 = np.array([0.0, 0.5, 1.0, 1.5, 2.0, 3.0, 4.0, 6.0, -0.0, -0.5, -1.0, -1.5, -2.0, -3.0, -4.0, -6.0])


def pack_weight(w, fmt):
    k, n = w.shape
    w = f64(np.asarray(w, np.float32).astype(ml_dtypes.bfloat16)).reshape(k // 32, 32, n)
    amax = np.abs(w).max(1)
    if fmt == "e4m3":
        byte = np.frexp(amax)[1] - 1 + 127 - 7
    else:
        mant, ex = np.frexp(amax / 6.0)
        byte = np.where(mant > 0.5, ex, ex - 1) + 127
    byte = np.clip(np.where(amax > 0, byte, 1), 1, 254)
    scaled = (w * np.exp2(127.0 - byte)[:, None, :]).reshape(k, n).astype(np.float32)
    by_word = np.ascontiguousarray(scaled.reshape(k // 512, 128, 4, n).transpose(0, 1, 3, 2))
    if fmt == "e4m3":
        words = by_word.astype(ml_dtypes.float8_e4m3fn).view(np.uint8)
    else:
        c = by_word.astype(ml_dtypes.float4_e2m1fn).view(np.uint8) & 0xF
        words = (c[..., 0::2] | (c[..., 1::2] << 4)).reshape(k // 512, 128, 2 * n)
    return np.ascontiguousarray(words), np.ascontiguousarray(byte.astype(np.uint8).reshape(k // 512, 16, n))


def unpack_weight(words, scales, fmt):
    g, _, n = scales.shape
    words = np.ascontiguousarray(words).reshape(g, 128, n, -1)
    if fmt == "e4m3":
        vals = words.view(ml_dtypes.float8_e4m3fn).astype(np.float64)
    else:
        nib = np.empty((g, 128, n, 4), np.uint8)
        nib[..., 0::2] = words & 0xF
        nib[..., 1::2] = words >> 4
        vals = E2M1[nib]
    vals = vals * np.repeat(np.exp2(scales.astype(np.float64) - 127.0), 8, axis=1)[..., None]
    return vals.transpose(0, 1, 3, 2).reshape(g * 512, n)


D, T, I, Q, E = 512, 1024, 512, 512, 256


def setup_inputs():
    n = np.random.standard_normal
    idx = np.stack([np.random.permutation(T)[:I] for _ in range(8)])
    idx2 = np.stack([np.random.permutation(I)[:I] for _ in range(8)])
    idx3 = np.stack([np.random.permutation(T)[:I] for _ in range(8)])
    idx4 = np.stack([np.random.permutation(T)[:I] for _ in range(8)])
    fd = mx_kscale(D)
    fq = mx_kscale(Q)
    keysp = pack_weight(n((D, T)) / fd[:, None], "e2m1")
    mixp = pack_weight(n((Q, E)) * 1.0 / np.sqrt(Q) / fq[:, None], "e4m3")
    return {
        "query": (n((D, Q)) * 1.0 / np.sqrt(D) * fd[:, None]).astype(np.float32),
        "keys_words": keysp[0],
        "keys_scales": keysp[1],
        "rowf": (np.random.uniform(0.5, 2.0, (Q, 1)) * fq[:, None]).astype(np.float32),
        "mix_words": mixp[0],
        "mix_scales": mixp[1],
        "offs": striped8(idx),
        "offs2": striped8(idx2),
        "offs3": striped8(idx3),
        "offs4": striped8(idx4),
    }


def reference(query, keys_words, keys_scales, rowf, mix_words, mix_scales, offs, offs2, offs3, offs4):
    idx = unstriped8(offs)
    idx2 = unstriped8(offs2)
    idx3 = unstriped8(offs3)
    idx4 = unstriped8(offs4)
    keysu = unpack_weight(keys_words, keys_scales, "e2m1")
    mixu = unpack_weight(mix_words, mix_scales, "e4m3")
    queryq = mxq(f64(query), 0, "e4m3")
    a = queryq.T @ keysu
    w = pick8(a, idx, 64) * 1.25
    v = pick8(w, idx2, 64)
    m1 = np.maximum(w, v)
    f1 = np.zeros((Q, T))
    f1[np.arange(Q)[:, None], idx3[np.arange(Q) % 512 // 64]] = m1
    c1 = a - f1
    g = pick8(c1, idx4, 64) + v
    gw = g * f64(rowf)
    gwq = mxq(gw, 0, "e4m3")
    y = mixu.T @ gwq
    return y

@@ -1,0 +1,215 @@
+from contextlib import ExitStack
+
+import concourse.mybir as mybir
+
+D, T, I, Q, E = 512, 1024, 512, 512, 256
+P = 128
+PACK = 4
+BANK = 512
+
+F32 = mybir.dt.float32
+BF16 = mybir.dt.bfloat16
+U32 = mybir.dt.uint32
+I32 = mybir.dt.int32
+U16 = mybir.dt.uint16
+U8 = mybir.dt.uint8
+FP8X4 = mybir.dt.float8_e4m3fn_x4
+FP4X4 = mybir.dt.float4_e2m1fn_x4
+ALU = mybir.AluOpType
+COPY = mybir.ActivationFunctionType.Copy
+
+FLOPS = 2 * D * Q * T + 2 * Q * E * I
+W_FACTOR = 1.25
+
+
+def tile_attend_slotmix_one_mixed_kernel(tc, query, keys_words, keys_scales, rowf, mix_words, mix_scales, offs, offs2, offs3, offs4, out):
+    nc = tc.nc
+    half = I // 2
+    cols = I // 16
+    with ExitStack() as ctx:
+        lists = ctx.enter_context(tc.tile_pool(name="lists", bufs=1))
+        keep = ctx.enter_context(tc.tile_pool(name="keep", bufs=1))
+        shared = ctx.enter_context(tc.tile_pool(name="shared", bufs=1))
+        psum = ctx.enter_context(tc.psum_pool(name="psum", bufs=2))
+
+        idx = lists.tile([P, cols], U16, name="idx")
+        idx2 = lists.tile([P, cols], U16, name="idx2")
+        idx3 = lists.tile([P, cols], U16, name="idx3")
+        idx4 = lists.tile([P, cols], U16, name="idx4")
+
+        key_scale = keep.tile([P, T], U8, name="key_scale", align_bytes=64)
+        mix_scale = keep.tile([P, E], U8, name="mix_scale", align_bytes=64)
+        nc.vector.memset(key_scale[:].bitcast(I32), 0)
+        nc.vector.memset(mix_scale[:].bitcast(I32), 0)
+
+        q_view = query.rearrange("(p j) q -> p j q", j=PACK)
+        q_raw = [keep.tile([P, PACK, Q // 2], F32, name="q_raw%d" % u) for u in range(2)]
+        for u in range(2):
+            nc.sync.dma_start(out=q_raw[u][:], in_=q_view[:, :, u * (Q // 2) : (u + 1) * (Q // 2)])
+        for quad in range(4):
+            nc.scalar.dma_start(out=key_scale[32 * quad : 32 * quad + 4, :].bitcast(I32), in_=keys_scales[0, 4 * quad : 4 * quad + 4, :].bitcast(I32))
+        key_code = keep.tile([P, 2 * T], U8, name="key_code", align_bytes=64)
+        nc.sync.dma_start(out=key_code[:].bitcast(I32), in_=keys_words[0].bitcast(I32))
+        nc.sync.dma_start(idx[:], offs)
+        nc.sync.dma_start(idx2[:], offs2)
+        nc.sync.dma_start(idx3[:], offs3)
+        nc.sync.dma_start(idx4[:], offs4)
+        row_factor = keep.tile([P, PACK], F32, name="row_factor")
+        nc.sync.dma_start(out=row_factor[:], in_=rowf.rearrange("(p t) o -> p (t o)", t=PACK))
+        mix_code = keep.tile([P, E], U32, name="mix_code", align_bytes=64)
+        nc.sync.dma_start(out=mix_code[:].bitcast(I32), in_=mix_words[0].rearrange("p e r -> p (e r)").bitcast(I32))
+        for quad in range(4):
+            nc.sync.dma_start(out=mix_scale[32 * quad : 32 * quad + 4, :].bitcast(I32), in_=mix_scales[0, 4 * quad : 4 * quad + 4, :].bitcast(I32))
+
+        f1 = [keep.tile([P, T], F32, name="f1_%d" % b) for b in range(2)]
+        for b in range(2):
+            nc.vector.memset(f1[b][:], 0.0)
+
+        q_bf = keep.tile([P, PACK, P, PACK], BF16, name="q_bf", align_bytes=64)
+        for u in range(2):
+            nc.vector.tensor_copy(
+                out=q_bf[:, :, u * (P // 2) : (u + 1) * (P // 2), :].rearrange("p t m j -> p m j t"),
+                in_=q_raw[u][:].rearrange("p j (m t) -> p m j t", t=PACK),
+            )
+
+        q_codes, q_scales = [], []
+        for t in range(PACK):
+            q_code = keep.tile([P, P], U32, name="q_code%d" % t, align_bytes=64)
+            q_scale = keep.tile([P, P], U8, name="q_scale%d" % t, align_bytes=64)
+            nc.vector.quantize_mx(out=q_code[:].bitcast(FP8X4), scales=q_scale[:], in_=q_bf[:, t].rearrange("p m j -> p (m j)"))
+            q_codes.append(q_code)
+            q_scales.append(q_scale)
+
+        def part(list_tile, h):
+            return list_tile[:, h * (cols // 2) : (h + 1) * (cols // 2)]
+
+        KB = 1024
+        last = PACK - 1
+        lo, hi = slice(0, half), slice(half, I)
+        a = [keep.tile([P, T], F32, name="a%d" % t) for t in range(PACK)]
+        m1 = [keep.tile([P, I], F32, name="m1_%d" % t) for t in range(PACK)]
+        g = [keep.tile([P, I], F32, name="g%d" % t) for t in range(PACK)]
+        w_at = {1: 0, 2: 7 * KB, 3: 12 * KB}
+        c1_at = {0: 0, 1: 4 * KB, 2: 9 * KB}
+        w, v, c1, picked, banks = {}, {}, {}, {}, {}
+
+        def scores(t):
+            banks[t] = []
+            for n in range(2):
+                bank = psum.tile([P, BANK], F32, name="score_bank", tag="score_bank")
+                nc.tensor.matmul_mx(
+                    out=bank[:],
+                    lhsT=q_codes[t][:].bitcast(FP8X4),
+                    lhsT_scale=q_scales[t][:],
+                    rhs=key_code[:, 2 * BANK * n : 2 * BANK * (n + 1)].bitcast(FP4X4),
+                    rhs_scale=key_scale[:, BANK * n : BANK * (n + 1)],
+                    start=True,
+                    stop=True,
+                )
+                banks[t].append(bank)
+
+        def look_w(t):
+            for n in range(2):
+                nc.scalar.copy(out=a[t][:, n * BANK : (n + 1) * BANK], in_=banks[t][n][:])
+            w[t] = shared.tile([P, I], F32, name="w%d" % t, offset=w_at[t])
+            nc.scalar.activation(w[t][:], a[t][:].indirect(idx[:]), COPY, scale=W_FACTOR)
+
+        def look_v(t):
+            if t == last:
+                v[t] = shared.tile([P, I], F32, name="v%d" % t, offset=0)
+            else:
+                v[t] = keep.tile([P, I], F32, name="v%d" % t)
+            nc.scalar.activation(v[t][:, lo], w[t][:].indirect(part(idx2, 0)), COPY)
+            nc.scalar.activation(v[t][:, hi], w[t][:].indirect(part(idx2, 1)), COPY)
+
+        def larger(t):
+            nc.vector.tensor_tensor(m1[t][:], w[t][:], v[t][:], ALU.max)
+
+        def scatter(t):
+            nc.vector.tensor_copy(f1[t % 2][:].indirect(idx3[:]), m1[t][:])
+
+        def take_off(t):
+            c1[t] = shared.tile([P, T], F32, name="c1_%d" % t, offset=c1_at[t])
+            nc.gpsimd.tensor_tensor(c1[t][:], a[t][:], f1[t % 2][:], ALU.subtract)
+
+        def look_c(t, dest):
+            nc.scalar.activation(dest, c1[t][:].indirect(idx4[:]), COPY)
+            nc.gpsimd.tensor_tensor(g[t][:], dest, v[t][:], ALU.add)
+
+        def scale(t):
+            for h in range(2):
+                nc.scalar.activation(gw[h][:, t, :], g[t][:, h * half : (h + 1) * half], COPY, scale=row_factor[:, t : t + 1])
+
+        scores(0)
+        w[0] = keep.tile([P, I], F32, name="w0")
+        v[0] = keep.tile([P, I], F32, name="v0")
+        nc.vector.tensor_copy(out=a[0][:, :BANK], in_=banks[0][0][:])
+        nc.scalar.copy(out=a[0][:, BANK:], in_=banks[0][1][:])
+        nc.vector.tensor_scalar(w[0][:, lo], a[0][:].indirect(part(idx, 0)), W_FACTOR, 0.0, ALU.mult, ALU.add)
+        nc.scalar.activation(w[0][:, hi], a[0][:].indirect(part(idx, 1)), COPY, scale=W_FACTOR)
+        nc.vector.tensor_copy(v[0][:, lo], w[0][:].indirect(part(idx2, 0)))
+        nc.scalar.activation(v[0][:, hi], w[0][:].indirect(part(idx2, 1)), COPY)
+        larger(0)
+        scatter(0)
+        for t in (1, 2):
+            scores(t)
+            look_w(t)
+            look_v(t)
+            larger(t)
+            take_off(t - 1)
+            scatter(t)
+        scores(last)
+        look_w(last)
+        picked0 = shared.tile([P, I], F32, name="picked0", offset=8 * KB)
+        look_c(0, picked0[:])
+        look_v(last)
+        larger(last)
+        take_off(2)
+        scatter(last)
+        late = shared.tile([P, 2 * PACK * half + I], F32, name="late", offset=13 * KB)
+        gw = [late[:, h * PACK * half : (h + 1) * PACK * half].rearrange("p (t i) -> p t i", t=PACK) for h in range(2)]
+        look_c(1, late[:, 2 * PACK * half :])
+        scale(0)
+        picked2 = keep.tile([P, I], F32, name="picked2")
+        look_c(2, picked2[:])
+        scale(1)
+
+        t = last
+        c1[t] = keep.tile([P, T], F32, name="c1_3")
+        for n in range(2):
+            nc.vector.tensor_tensor(c1[t][:, n * BANK : (n + 1) * BANK], banks[t][n][:], f1[t % 2][:, n * BANK : (n + 1) * BANK], ALU.subtract)
+        picked3 = shared.tile([P, half], F32, name="picked3", offset=10 * KB)
+        nc.vector.tensor_tensor(g[t][:, lo], c1[t][:].indirect(part(idx4, 0)), v[t][:, lo], ALU.add)
+        nc.scalar.activation(picked3[:], c1[t][:].indirect(part(idx4, 1)), COPY)
+        scale(2)
+        nc.vector.tensor_scalar(gw[0][:, t, :], g[t][:, lo], row_factor[:, t : t + 1], None, ALU.mult)
+        nc.vector.tensor_tensor(g[t][:, hi], picked3[:], v[t][:, hi], ALU.add)
+        nc.scalar.activation(gw[1][:, t, :], g[t][:, hi], COPY, scale=row_factor[:, t : t + 1])
+
+        out_view = out.rearrange("(m p) i -> p m i", p=P)
+        for h in range(2):
+            gw_bf = keep.tile([P, half, PACK], BF16, name="gw_bf%d" % h, align_bytes=64)
+            nc.vector.tensor_copy(
+                out=gw_bf[:].rearrange("p (c i) t -> p c t i", i=4),
+                in_=gw[h].rearrange("p t (c i) -> p c t i", i=4),
+            )
+            gw_code = keep.tile([P, half], U32, name="gw_code%d" % h, align_bytes=64)
+            gw_scale = keep.tile([P, half], U8, name="gw_scale%d" % h, align_bytes=64)
+            nc.vector.quantize_mx(out=gw_code[:].bitcast(FP8X4), scales=gw_scale[:], in_=gw_bf[:].rearrange("p i t -> p (i t)"))
+            result = keep.tile([P, 2, half], F32, name="result%d" % h)
+            for m in range(2):
+                bank = psum.tile([P, BANK], F32, name="out_bank", tag="out_bank", bufs=4)
+                nc.tensor.matmul_mx(
+                    out=bank[:, :half],
+                    lhsT=mix_code[:, m * P : (m + 1) * P].bitcast(FP8X4),
+                    lhsT_scale=mix_scale[:, m * P : (m + 1) * P],
+                    rhs=gw_code[:].bitcast(FP8X4),
+                    rhs_scale=gw_scale[:],
+                    start=True,
+                    stop=True,
+                )
+                if h == 1 and m == 1:
+                    nc.vector.tensor_copy(out=result[:, m, :], in_=bank[:, :half])
+                else:
+                    nc.scalar.copy(out=result[:, m, :], in_=bank[:, :half])
+            nc.sync.dma_start(out=out_view[:, :, h * half : (h + 1) * half], in_=result[:])

@@ -4,8 +4,14 @@ import concourse.mybir as mybir
 
 D, T, I, Q, E = 512, 1024, 512, 512, 256
 P = 128
-PACK = 4
+PLACES = 4
 BANK = 512
+PIECE = 256
+SPAN = 128
+HALF = I // 2
+LIST_COLS = I // 16
+W_FACTOR = 1.25
+KB = 1024
 
 F32 = mybir.dt.float32
 BF16 = mybir.dt.bfloat16
@@ -19,108 +25,114 @@ ALU = mybir.AluOpType
 COPY = mybir.ActivationFunctionType.Copy
 
 FLOPS = 2 * D * Q * T + 2 * Q * E * I
-W_FACTOR = 1.25
 
 
-def tile_attend_slotmix_one_mixed_kernel(tc, query, keys_words, keys_scales, rowf, mix_words, mix_scales, offs, offs2, offs3, offs4, out):
+def tile_attend_slotmix_one_mixed_kernel(
+    tc, query, keys_words, keys_scales, rowf, mix_words, mix_scales, offs, offs2, offs3, offs4, out
+):
     nc = tc.nc
-    half = I // 2
-    cols = I // 16
+    last = PLACES - 1
+    halves = (slice(0, HALF), slice(HALF, I))
+    lo, hi = halves
     with ExitStack() as ctx:
         lists = ctx.enter_context(tc.tile_pool(name="lists", bufs=1))
         keep = ctx.enter_context(tc.tile_pool(name="keep", bufs=1))
         shared = ctx.enter_context(tc.tile_pool(name="shared", bufs=1))
-        psum = ctx.enter_context(tc.psum_pool(name="psum", bufs=2))
+        psum = ctx.enter_context(tc.psum_pool(name="psum", bufs=8))
 
-        idx = lists.tile([P, cols], U16, name="idx")
-        idx2 = lists.tile([P, cols], U16, name="idx2")
-        idx3 = lists.tile([P, cols], U16, name="idx3")
-        idx4 = lists.tile([P, cols], U16, name="idx4")
+        idx = lists.tile([P, LIST_COLS], U16, name="idx")
+        idx2 = lists.tile([P, LIST_COLS], U16, name="idx2")
+        idx3 = lists.tile([P, LIST_COLS], U16, name="idx3")
+        idx4 = lists.tile([P, LIST_COLS], U16, name="idx4")
 
-        key_scale = keep.tile([P, T], U8, name="key_scale", align_bytes=64)
-        mix_scale = keep.tile([P, E], U8, name="mix_scale", align_bytes=64)
-        nc.vector.memset(key_scale[:].bitcast(I32), 0)
-        nc.vector.memset(mix_scale[:].bitcast(I32), 0)
+        def half_list(list_tile, h):
+            return list_tile[:, h * (LIST_COLS // 2) : (h + 1) * (LIST_COLS // 2)]
 
-        q_view = query.rearrange("(p j) q -> p j q", j=PACK)
-        q_raw = [keep.tile([P, PACK, Q // 2], F32, name="q_raw%d" % u) for u in range(2)]
+        def load_scale_rows(queue, plane, rows):
+            for quad in range(4):
+                queue.dma_start(
+                    out=plane[32 * quad : 32 * quad + 4, :].bitcast(I32),
+                    in_=rows[0, 4 * quad : 4 * quad + 4, :].bitcast(I32),
+                )
+
+        q_view = query.rearrange("(p j) q -> p j q", j=PLACES)
+        q_raw = [keep.tile([P, PLACES, Q // 2], F32, name="q_raw%d" % u) for u in range(2)]
         for u in range(2):
             nc.sync.dma_start(out=q_raw[u][:], in_=q_view[:, :, u * (Q // 2) : (u + 1) * (Q // 2)])
-        for quad in range(4):
-            nc.scalar.dma_start(out=key_scale[32 * quad : 32 * quad + 4, :].bitcast(I32), in_=keys_scales[0, 4 * quad : 4 * quad + 4, :].bitcast(I32))
+        key_scale = keep.tile([P, T], U8, name="key_scale", align_bytes=64)
+        load_scale_rows(nc.scalar, key_scale, keys_scales)
         key_code = keep.tile([P, 2 * T], U8, name="key_code", align_bytes=64)
         nc.sync.dma_start(out=key_code[:].bitcast(I32), in_=keys_words[0].bitcast(I32))
         nc.sync.dma_start(idx[:], offs)
         nc.sync.dma_start(idx2[:], offs2)
         nc.sync.dma_start(idx3[:], offs3)
         nc.sync.dma_start(idx4[:], offs4)
-        row_factor = keep.tile([P, PACK], F32, name="row_factor")
-        nc.sync.dma_start(out=row_factor[:], in_=rowf.rearrange("(p t) o -> p (t o)", t=PACK))
+        row_factor = keep.tile([P, PLACES], F32, name="row_factor")
+        nc.sync.dma_start(out=row_factor[:], in_=rowf.rearrange("(p t) o -> p (t o)", t=PLACES))
         mix_code = keep.tile([P, E], U32, name="mix_code", align_bytes=64)
         nc.sync.dma_start(out=mix_code[:].bitcast(I32), in_=mix_words[0].rearrange("p e r -> p (e r)").bitcast(I32))
-        for quad in range(4):
-            nc.sync.dma_start(out=mix_scale[32 * quad : 32 * quad + 4, :].bitcast(I32), in_=mix_scales[0, 4 * quad : 4 * quad + 4, :].bitcast(I32))
+        mix_scale = keep.tile([P, E], U8, name="mix_scale", align_bytes=64)
+        load_scale_rows(nc.sync, mix_scale, mix_scales)
 
         f1 = [keep.tile([P, T], F32, name="f1_%d" % b) for b in range(2)]
         for b in range(2):
             nc.vector.memset(f1[b][:], 0.0)
 
-        q_bf = keep.tile([P, PACK, P, PACK], BF16, name="q_bf", align_bytes=64)
+        q_first = keep.tile([P, P, PLACES], BF16, name="q_first", align_bytes=64)
+        q_rest = keep.tile([P, last, P, PLACES], BF16, name="q_rest", align_bytes=64)
         for u in range(2):
-            nc.vector.tensor_copy(
-                out=q_bf[:, :, u * (P // 2) : (u + 1) * (P // 2), :].rearrange("p t m j -> p m j t"),
-                in_=q_raw[u][:].rearrange("p j (m t) -> p m j t", t=PACK),
+            cols = slice(u * (P // 2), (u + 1) * (P // 2))
+            dealt = q_raw[u][:].rearrange("p j (m t) -> p m j t", t=PLACES)
+            nc.vector.tensor_copy(out=q_first[:, cols, :], in_=dealt[:, :, :, 0])
+            cast_rest = nc.vector.tensor_copy if u == 0 else nc.scalar.copy
+            cast_rest(out=q_rest[:, :, cols, :].rearrange("p t m j -> p m j t"), in_=dealt[:, :, :, 1:])
+
+        q_code, q_scale = [], []
+        for t in range(PLACES):
+            q_code.append(keep.tile([P, P], U32, name="q_code%d" % t, align_bytes=64))
+            q_scale.append(keep.tile([P, P], U8, name="q_scale%d" % t, align_bytes=64))
+            rounded = q_first[:] if t == 0 else q_rest[:, t - 1]
+            nc.vector.quantize_mx(
+                out=q_code[t][:].bitcast(FP8X4), scales=q_scale[t][:], in_=rounded.rearrange("p m j -> p (m j)")
             )
 
-        q_codes, q_scales = [], []
-        for t in range(PACK):
-            q_code = keep.tile([P, P], U32, name="q_code%d" % t, align_bytes=64)
-            q_scale = keep.tile([P, P], U8, name="q_scale%d" % t, align_bytes=64)
-            nc.vector.quantize_mx(out=q_code[:].bitcast(FP8X4), scales=q_scale[:], in_=q_bf[:, t].rearrange("p m j -> p (m j)"))
-            q_codes.append(q_code)
-            q_scales.append(q_scale)
+        w_at = {1: 0, 2: 4 * KB, 3: 15 * KB}
+        c1_at = {0: 0, 1: 4 * KB, 2: 12 * KB}
+        a2_at, g_late_at, scaled_at, a3_at = 8 * KB, 9 * KB, 16 * KB, 28 * KB
 
-        def part(list_tile, h):
-            return list_tile[:, h * (cols // 2) : (h + 1) * (cols // 2)]
+        a = [keep.tile([P, T], F32, name="a%d" % t) for t in range(2)]
+        a.append(shared.tile([P, T], F32, name="a2", offset=a2_at))
+        a.append(shared.tile([P, T], F32, name="a3", offset=a3_at))
+        m1 = [keep.tile([P, I], F32, name="m1_%d" % t) for t in range(PLACES)]
+        w, v, c1, score_banks = {}, {}, {}, {}
 
-        KB = 1024
-        last = PACK - 1
-        lo, hi = slice(0, half), slice(half, I)
-        a = [keep.tile([P, T], F32, name="a%d" % t) for t in range(PACK)]
-        m1 = [keep.tile([P, I], F32, name="m1_%d" % t) for t in range(PACK)]
-        g = [keep.tile([P, I], F32, name="g%d" % t) for t in range(PACK)]
-        w_at = {1: 0, 2: 7 * KB, 3: 12 * KB}
-        c1_at = {0: 0, 1: 4 * KB, 2: 9 * KB}
-        w, v, c1, picked, banks = {}, {}, {}, {}, {}
-
-        def scores(t):
-            banks[t] = []
-            for n in range(2):
-                bank = psum.tile([P, BANK], F32, name="score_bank", tag="score_bank")
+        def scores(t, width):
+            score_banks[t] = []
+            for n in range(T // width):
+                bank = psum.tile([P, width], F32, name="bank", tag="bank")
                 nc.tensor.matmul_mx(
                     out=bank[:],
-                    lhsT=q_codes[t][:].bitcast(FP8X4),
-                    lhsT_scale=q_scales[t][:],
-                    rhs=key_code[:, 2 * BANK * n : 2 * BANK * (n + 1)].bitcast(FP4X4),
-                    rhs_scale=key_scale[:, BANK * n : BANK * (n + 1)],
+                    lhsT=q_code[t][:].bitcast(FP8X4),
+                    lhsT_scale=q_scale[t][:],
+                    rhs=key_code[:, 2 * width * n : 2 * width * (n + 1)].bitcast(FP4X4),
+                    rhs_scale=key_scale[:, width * n : width * (n + 1)],
                     start=True,
                     stop=True,
                 )
-                banks[t].append(bank)
+                score_banks[t].append(bank)
+            for n in range(T // PIECE):
+                at = n * PIECE % width
+                leave_psum = nc.vector.tensor_copy if t == 0 and n % 2 == 0 else nc.scalar.copy
+                leave_psum(out=a[t][:, n * PIECE : (n + 1) * PIECE], in_=score_banks[t][n * PIECE // width][:, at : at + PIECE])
 
-        def look_w(t):
-            for n in range(2):
-                nc.scalar.copy(out=a[t][:, n * BANK : (n + 1) * BANK], in_=banks[t][n][:])
+        def look_up_w(t):
             w[t] = shared.tile([P, I], F32, name="w%d" % t, offset=w_at[t])
             nc.scalar.activation(w[t][:], a[t][:].indirect(idx[:]), COPY, scale=W_FACTOR)
 
-        def look_v(t):
-            if t == last:
-                v[t] = shared.tile([P, I], F32, name="v%d" % t, offset=0)
-            else:
-                v[t] = keep.tile([P, I], F32, name="v%d" % t)
-            nc.scalar.activation(v[t][:, lo], w[t][:].indirect(part(idx2, 0)), COPY)
-            nc.scalar.activation(v[t][:, hi], w[t][:].indirect(part(idx2, 1)), COPY)
+        def look_up_v(t):
+            v[t] = keep.tile([P, I], F32, name="v%d" % t)
+            for h in range(2):
+                nc.scalar.activation(v[t][:, halves[h]], w[t][:].indirect(half_list(idx2, h)), COPY)
 
         def larger(t):
             nc.vector.tensor_tensor(m1[t][:], w[t][:], v[t][:], ALU.max)
@@ -132,75 +144,108 @@ def tile_attend_slotmix_one_mixed_kernel(tc, query, keys_words, keys_scales, row
             c1[t] = shared.tile([P, T], F32, name="c1_%d" % t, offset=c1_at[t])
             nc.gpsimd.tensor_tensor(c1[t][:], a[t][:], f1[t % 2][:], ALU.subtract)
 
-        def look_c(t, dest):
-            nc.scalar.activation(dest, c1[t][:].indirect(idx4[:]), COPY)
-            nc.gpsimd.tensor_tensor(g[t][:], dest, v[t][:], ALU.add)
+        def add_v(t, h, picked, g_half):
+            nc.gpsimd.tensor_tensor(g_half, picked[:, halves[h]], v[t][:, halves[h]], ALU.add)
 
-        def scale(t):
-            for h in range(2):
-                nc.scalar.activation(gw[h][:, t, :], g[t][:, h * half : (h + 1) * half], COPY, scale=row_factor[:, t : t + 1])
-
-        scores(0)
+        scores(0, PIECE)
         w[0] = keep.tile([P, I], F32, name="w0")
         v[0] = keep.tile([P, I], F32, name="v0")
-        nc.vector.tensor_copy(out=a[0][:, :BANK], in_=banks[0][0][:])
-        nc.scalar.copy(out=a[0][:, BANK:], in_=banks[0][1][:])
-        nc.vector.tensor_scalar(w[0][:, lo], a[0][:].indirect(part(idx, 0)), W_FACTOR, 0.0, ALU.mult, ALU.add)
-        nc.scalar.activation(w[0][:, hi], a[0][:].indirect(part(idx, 1)), COPY, scale=W_FACTOR)
-        nc.vector.tensor_copy(v[0][:, lo], w[0][:].indirect(part(idx2, 0)))
-        nc.scalar.activation(v[0][:, hi], w[0][:].indirect(part(idx2, 1)), COPY)
+        nc.vector.tensor_scalar(w[0][:, lo], a[0][:].indirect(half_list(idx, 0)), W_FACTOR, 0.0, ALU.mult, ALU.add)
+        nc.scalar.activation(w[0][:, hi], a[0][:].indirect(half_list(idx, 1)), COPY, scale=W_FACTOR)
+        nc.vector.tensor_copy(v[0][:, lo], w[0][:].indirect(half_list(idx2, 0)))
+        nc.scalar.activation(v[0][:, hi], w[0][:].indirect(half_list(idx2, 1)), COPY)
         larger(0)
         scatter(0)
+
         for t in (1, 2):
-            scores(t)
-            look_w(t)
-            look_v(t)
+            scores(t, PIECE if t == 1 else BANK)
+            look_up_w(t)
+            look_up_v(t)
             larger(t)
             take_off(t - 1)
             scatter(t)
-        scores(last)
-        look_w(last)
-        picked0 = shared.tile([P, I], F32, name="picked0", offset=8 * KB)
-        look_c(0, picked0[:])
-        look_v(last)
-        larger(last)
-        take_off(2)
-        scatter(last)
-        late = shared.tile([P, 2 * PACK * half + I], F32, name="late", offset=13 * KB)
-        gw = [late[:, h * PACK * half : (h + 1) * PACK * half].rearrange("p (t i) -> p t i", t=PACK) for h in range(2)]
-        look_c(1, late[:, 2 * PACK * half :])
-        scale(0)
-        picked2 = keep.tile([P, I], F32, name="picked2")
-        look_c(2, picked2[:])
-        scale(1)
 
-        t = last
-        c1[t] = keep.tile([P, T], F32, name="c1_3")
-        for n in range(2):
-            nc.vector.tensor_tensor(c1[t][:, n * BANK : (n + 1) * BANK], banks[t][n][:], f1[t % 2][:, n * BANK : (n + 1) * BANK], ALU.subtract)
-        picked3 = shared.tile([P, half], F32, name="picked3", offset=10 * KB)
-        nc.vector.tensor_tensor(g[t][:, lo], c1[t][:].indirect(part(idx4, 0)), v[t][:, lo], ALU.add)
-        nc.scalar.activation(picked3[:], c1[t][:].indirect(part(idx4, 1)), COPY)
-        scale(2)
-        nc.vector.tensor_scalar(gw[0][:, t, :], g[t][:, lo], row_factor[:, t : t + 1], None, ALU.mult)
-        nc.vector.tensor_tensor(g[t][:, hi], picked3[:], v[t][:, hi], ALU.add)
-        nc.scalar.activation(gw[1][:, t, :], g[t][:, hi], COPY, scale=row_factor[:, t : t + 1])
+        scores(last, BANK)
+        look_up_w(last)
+        picked01 = shared.tile([P, 2, I], F32, name="picked01", offset=a3_at)
+        picked0, picked1 = picked01[:, 0, :], picked01[:, 1, :]
+        g0_lo = keep.tile([P, HALF], F32, name="g0_lo")
+        nc.scalar.activation(picked0[:, lo], c1[0][:].indirect(half_list(idx4, 0)), COPY)
+        add_v(0, 0, picked0, g0_lo[:])
+        look_up_v(last)
+        nc.scalar.activation(picked0[:, hi], c1[0][:].indirect(half_list(idx4, 1)), COPY)
+        larger(last)
+        take_off(last - 1)
+        scatter(last)
+
+        g_late = shared.tile([P, 3, HALF], F32, name="g_late", offset=g_late_at)
+        g0_hi, g1_lo, g1_hi = g_late[:, 0, :], g_late[:, 1, :], g_late[:, 2, :]
+        add_v(0, 1, picked0, g0_hi)
+        nc.scalar.activation(picked1, c1[1][:].indirect(idx4[:]), COPY)
+        add_v(1, 0, picked1, g1_lo)
+        add_v(1, 1, picked1, g1_hi)
+
+        scaled = shared.tile([P, 2 * PLACES * HALF + 2 * I], F32, name="scaled", offset=scaled_at)
+        gw = [
+            scaled[:, h * PLACES * HALF : (h + 1) * PLACES * HALF].rearrange("p (t i) -> p t i", t=PLACES)
+            for h in range(2)
+        ]
+        v_scaled = {t: scaled[:, 2 * PLACES * HALF + (t - 2) * I : 2 * PLACES * HALF + (t - 1) * I] for t in (2, 3)}
+
+        def times_rowf(t, dest, source):
+            nc.scalar.activation(dest, source, COPY, scale=row_factor[:, t : t + 1])
+
+        def scale_and_add(t, h, picked_half):
+            nc.vector.scalar_tensor_tensor(
+                gw[h][:, t, :], picked_half, row_factor[:, t : t + 1], v_scaled[t][:, halves[h]], ALU.mult, ALU.add
+            )
+
+        times_rowf(0, gw[0][:, 0, :], g0_lo[:])
+        for t in (2, 3):
+            times_rowf(t, v_scaled[t], v[t][:])
+        picked2 = keep.tile([P, I], F32, name="picked2")
+        nc.scalar.activation(picked2[:], c1[2][:].indirect(idx4[:]), COPY)
+        times_rowf(0, gw[1][:, 0, :], g0_hi)
+        times_rowf(1, gw[0][:, 1, :], g1_lo)
+        times_rowf(1, gw[1][:, 1, :], g1_hi)
+
+        c1[last] = keep.tile([P, T], F32, name="c1_3")
+        for n in range(T // BANK):
+            cols = slice(n * BANK, (n + 1) * BANK)
+            nc.vector.tensor_tensor(c1[last][:, cols], score_banks[last][n][:], f1[last % 2][:, cols], ALU.subtract)
+        picked3_lo = keep.tile([P, HALF], F32, name="picked3_lo")
+        picked3_hi = shared.tile([P, HALF], F32, name="picked3_hi", offset=g_late_at)
+        scale_and_add(2, 0, picked2[:, lo])
+        nc.vector.tensor_copy(picked3_lo[:], c1[last][:].indirect(half_list(idx4, 0)))
+        nc.scalar.activation(picked3_hi[:], c1[last][:].indirect(half_list(idx4, 1)), COPY)
+        scale_and_add(2, 1, picked2[:, hi])
+        scale_and_add(last, 0, picked3_lo[:])
+        scale_and_add(last, 1, picked3_hi[:])
 
         out_view = out.rearrange("(m p) i -> p m i", p=P)
-        for h in range(2):
-            gw_bf = keep.tile([P, half, PACK], BF16, name="gw_bf%d" % h, align_bytes=64)
-            nc.vector.tensor_copy(
-                out=gw_bf[:].rearrange("p (c i) t -> p c t i", i=4),
-                in_=gw[h].rearrange("p t (c i) -> p c t i", i=4),
+        n_spans = I // SPAN
+        gw_bf = {}
+
+        def weave(n):
+            gw_bf[n] = keep.tile([P, SPAN, PLACES], BF16, name="gw_bf%d" % n, align_bytes=64)
+            at = n * SPAN % HALF
+            round_and_weave = nc.scalar.copy if n * SPAN == HALF else nc.vector.tensor_copy
+            round_and_weave(
+                out=gw_bf[n][:].rearrange("p (c i) t -> p c t i", i=4),
+                in_=gw[n * SPAN // HALF][:, :, at : at + SPAN].rearrange("p t (c i) -> p c t i", i=4),
             )
-            gw_code = keep.tile([P, half], U32, name="gw_code%d" % h, align_bytes=64)
-            gw_scale = keep.tile([P, half], U8, name="gw_scale%d" % h, align_bytes=64)
-            nc.vector.quantize_mx(out=gw_code[:].bitcast(FP8X4), scales=gw_scale[:], in_=gw_bf[:].rearrange("p i t -> p (i t)"))
-            result = keep.tile([P, 2, half], F32, name="result%d" % h)
-            for m in range(2):
-                bank = psum.tile([P, BANK], F32, name="out_bank", tag="out_bank", bufs=4)
+
+        def mix_rows(n):
+            gw_code = keep.tile([P, SPAN], U32, name="gw_code%d" % n, align_bytes=64)
+            gw_scale = keep.tile([P, SPAN], U8, name="gw_scale%d" % n, align_bytes=64)
+            nc.vector.quantize_mx(
+                out=gw_code[:].bitcast(FP8X4), scales=gw_scale[:], in_=gw_bf[n][:].rearrange("p i t -> p (i t)")
+            )
+            result = keep.tile([P, E // P, SPAN], F32, name="result%d" % n)
+            for m in range(E // P):
+                bank = psum.tile([P, SPAN], F32, name="bank", tag="bank")
                 nc.tensor.matmul_mx(
-                    out=bank[:, :half],
+                    out=bank[:],
                     lhsT=mix_code[:, m * P : (m + 1) * P].bitcast(FP8X4),
                     lhsT_scale=mix_scale[:, m * P : (m + 1) * P],
                     rhs=gw_code[:].bitcast(FP8X4),
@@ -208,8 +253,12 @@ def tile_attend_slotmix_one_mixed_kernel(tc, query, keys_words, keys_scales, row
                     start=True,
                     stop=True,
                 )
-                if h == 1 and m == 1:
-                    nc.vector.tensor_copy(out=result[:, m, :], in_=bank[:, :half])
-                else:
-                    nc.scalar.copy(out=result[:, m, :], in_=bank[:, :half])
-            nc.sync.dma_start(out=out_view[:, :, h * half : (h + 1) * half], in_=result[:])
+                leave_psum = nc.vector.tensor_copy if n == n_spans - 1 and m == 1 else nc.scalar.copy
+                leave_psum(out=result[:, m, :], in_=bank[:])
+            nc.sync.dma_start(out=out_view[:, :, n * SPAN : (n + 1) * SPAN], in_=result[:])
+
+        weave(0)
+        for n in range(1, n_spans):
+            weave(n)
+            mix_rows(n - 1)
+        mix_rows(n_spans - 1)

@@ -96,15 +96,17 @@ def tile_attend_slotmix_one_mixed_kernel(
                 out=q_code[t][:].bitcast(FP8X4), scales=q_scale[t][:], in_=rounded.rearrange("p m j -> p (m j)")
             )
 
-        w_at = {1: 0, 2: 4 * KB, 3: 15 * KB}
+        w_at = {1: 0, 2: 7 * KB, 3: 15 * KB}
         c1_at = {0: 0, 1: 4 * KB, 2: 12 * KB}
-        a2_at, g_late_at, scaled_at, a3_at = 8 * KB, 9 * KB, 16 * KB, 28 * KB
+        scaled_at, a3_at = 16 * KB, 32 * KB
 
-        a = [keep.tile([P, T], F32, name="a%d" % t) for t in range(2)]
-        a.append(shared.tile([P, T], F32, name="a2", offset=a2_at))
+        a = [keep.tile([P, T], F32, name="a%d" % t) for t in range(last)]
         a.append(shared.tile([P, T], F32, name="a3", offset=a3_at))
         m1 = [keep.tile([P, I], F32, name="m1_%d" % t) for t in range(PLACES)]
-        w, v, c1, score_banks = {}, {}, {}, {}
+        w, c1, score_banks = {}, {}, {}
+        v01 = keep.tile([P, 2 * I], F32, name="v01")
+        v = {0: v01[:, :I], 1: v01[:, I:]}
+        v.update({t: keep.tile([P, I], F32, name="v%d" % t)[:] for t in (2, 3)})
 
         def scores(t, width):
             score_banks[t] = []
@@ -130,7 +132,6 @@ def tile_attend_slotmix_one_mixed_kernel(
             nc.scalar.activation(w[t][:], a[t][:].indirect(idx[:]), COPY, scale=W_FACTOR)
 
         def look_up_v(t):
-            v[t] = keep.tile([P, I], F32, name="v%d" % t)
             for h in range(2):
                 nc.scalar.activation(v[t][:, halves[h]], w[t][:].indirect(half_list(idx2, h)), COPY)
 
@@ -144,12 +145,8 @@ def tile_attend_slotmix_one_mixed_kernel(
             c1[t] = shared.tile([P, T], F32, name="c1_%d" % t, offset=c1_at[t])
             nc.gpsimd.tensor_tensor(c1[t][:], a[t][:], f1[t % 2][:], ALU.subtract)
 
-        def add_v(t, h, picked, g_half):
-            nc.gpsimd.tensor_tensor(g_half, picked[:, halves[h]], v[t][:, halves[h]], ALU.add)
-
         scores(0, PIECE)
         w[0] = keep.tile([P, I], F32, name="w0")
-        v[0] = keep.tile([P, I], F32, name="v0")
         nc.vector.tensor_scalar(w[0][:, lo], a[0][:].indirect(half_list(idx, 0)), W_FACTOR, 0.0, ALU.mult, ALU.add)
         nc.scalar.activation(w[0][:, hi], a[0][:].indirect(half_list(idx, 1)), COPY, scale=W_FACTOR)
         nc.vector.tensor_copy(v[0][:, lo], w[0][:].indirect(half_list(idx2, 0)))
@@ -167,83 +164,82 @@ def tile_attend_slotmix_one_mixed_kernel(
 
         scores(last, BANK)
         look_up_w(last)
-        picked01 = shared.tile([P, 2, I], F32, name="picked01", offset=a3_at)
-        picked0, picked1 = picked01[:, 0, :], picked01[:, 1, :]
+        picked0_lo = shared.tile([P, HALF], F32, name="picked0_lo", offset=8 * KB)
         g0_lo = keep.tile([P, HALF], F32, name="g0_lo")
-        nc.scalar.activation(picked0[:, lo], c1[0][:].indirect(half_list(idx4, 0)), COPY)
-        add_v(0, 0, picked0, g0_lo[:])
+        nc.scalar.activation(picked0_lo[:], c1[0][:].indirect(half_list(idx4, 0)), COPY)
+        nc.gpsimd.tensor_tensor(g0_lo[:], picked0_lo[:], v[0][:, lo], ALU.add)
         look_up_v(last)
-        nc.scalar.activation(picked0[:, hi], c1[0][:].indirect(half_list(idx4, 1)), COPY)
+        picked_late = shared.tile([P, HALF + I], F32, name="picked_late", offset=a3_at)
+        picked0_hi, picked1 = picked_late[:, :HALF], picked_late[:, HALF:]
+        nc.scalar.activation(picked0_hi, c1[0][:].indirect(half_list(idx4, 1)), COPY)
         larger(last)
         take_off(last - 1)
         scatter(last)
 
-        g_late = shared.tile([P, 3, HALF], F32, name="g_late", offset=g_late_at)
-        g0_hi, g1_lo, g1_hi = g_late[:, 0, :], g_late[:, 1, :], g_late[:, 2, :]
-        add_v(0, 1, picked0, g0_hi)
-        nc.scalar.activation(picked1, c1[1][:].indirect(idx4[:]), COPY)
-        add_v(1, 0, picked1, g1_lo)
-        add_v(1, 1, picked1, g1_hi)
-
-        scaled = shared.tile([P, 2 * PLACES * HALF + 2 * I], F32, name="scaled", offset=scaled_at)
+        scaled = shared.tile([P, PLACES * I + 2 * I + HALF + I], F32, name="scaled", offset=scaled_at)
         gw = [
             scaled[:, h * PLACES * HALF : (h + 1) * PLACES * HALF].rearrange("p (t i) -> p t i", t=PLACES)
             for h in range(2)
         ]
-        v_scaled = {t: scaled[:, 2 * PLACES * HALF + (t - 2) * I : 2 * PLACES * HALF + (t - 1) * I] for t in (2, 3)}
+        v_scaled = {t: scaled[:, (PLACES + t - 2) * I : (PLACES + t - 1) * I] for t in (2, 3)}
+        g_late = scaled[:, (PLACES + 2) * I :]
+        g0_hi, g1 = g_late[:, :HALF], g_late[:, HALF:]
 
         def times_rowf(t, dest, source):
             nc.scalar.activation(dest, source, COPY, scale=row_factor[:, t : t + 1])
 
-        def scale_and_add(t, h, picked_half):
+        def scale_and_add(t, h, picked):
             nc.vector.scalar_tensor_tensor(
-                gw[h][:, t, :], picked_half, row_factor[:, t : t + 1], v_scaled[t][:, halves[h]], ALU.mult, ALU.add
+                gw[h][:, t, :], picked[:, halves[h]], row_factor[:, t : t + 1], v_scaled[t][:, halves[h]], ALU.mult, ALU.add
             )
 
+        nc.scalar.activation(picked1, c1[1][:].indirect(idx4[:]), COPY)
+        nc.gpsimd.tensor_tensor(g_late, picked_late[:], v01[:, HALF:], ALU.add)
         times_rowf(0, gw[0][:, 0, :], g0_lo[:])
         for t in (2, 3):
             times_rowf(t, v_scaled[t], v[t][:])
         picked2 = keep.tile([P, I], F32, name="picked2")
         nc.scalar.activation(picked2[:], c1[2][:].indirect(idx4[:]), COPY)
-        times_rowf(0, gw[1][:, 0, :], g0_hi)
-        times_rowf(1, gw[0][:, 1, :], g1_lo)
-        times_rowf(1, gw[1][:, 1, :], g1_hi)
 
         c1[last] = keep.tile([P, T], F32, name="c1_3")
         for n in range(T // BANK):
             cols = slice(n * BANK, (n + 1) * BANK)
             nc.vector.tensor_tensor(c1[last][:, cols], score_banks[last][n][:], f1[last % 2][:, cols], ALU.subtract)
-        picked3_lo = keep.tile([P, HALF], F32, name="picked3_lo")
-        picked3_hi = shared.tile([P, HALF], F32, name="picked3_hi", offset=g_late_at)
-        scale_and_add(2, 0, picked2[:, lo])
-        nc.vector.tensor_copy(picked3_lo[:], c1[last][:].indirect(half_list(idx4, 0)))
-        nc.scalar.activation(picked3_hi[:], c1[last][:].indirect(half_list(idx4, 1)), COPY)
-        scale_and_add(2, 1, picked2[:, hi])
-        scale_and_add(last, 0, picked3_lo[:])
-        scale_and_add(last, 1, picked3_hi[:])
+        picked3 = shared.tile([P, I], F32, name="picked3", offset=c1_at[2])
+        nc.scalar.activation(picked3[:, lo], c1[last][:].indirect(half_list(idx4, 0)), COPY)
+        nc.scalar.activation(picked3[:, hi], c1[last][:].indirect(half_list(idx4, 1)), COPY)
+        times_rowf(1, gw[0][:, 1, :], g1[:, lo])
+        times_rowf(1, gw[1][:, 1, :], g1[:, hi])
+        times_rowf(0, gw[1][:, 0, :], g0_hi)
+        scale_and_add(2, 0, picked2)
+        scale_and_add(2, 1, picked2)
+        scale_and_add(last, 0, picked3)
+        scale_and_add(last, 1, picked3)
 
         out_view = out.rearrange("(m p) i -> p m i", p=P)
-        n_spans = I // SPAN
+        spans = [(0, 256), (256, 128), (384, 128)]
+        n_spans = len(spans)
         gw_bf = {}
 
         def weave(n):
-            gw_bf[n] = keep.tile([P, SPAN, PLACES], BF16, name="gw_bf%d" % n, align_bytes=64)
-            at = n * SPAN % HALF
-            round_and_weave = nc.scalar.copy if n * SPAN == HALF else nc.vector.tensor_copy
+            start, width = spans[n]
+            gw_bf[n] = keep.tile([P, width, PLACES], BF16, name="gw_bf%d" % n, align_bytes=64)
+            round_and_weave = nc.scalar.copy if n == 1 else nc.vector.tensor_copy
             round_and_weave(
                 out=gw_bf[n][:].rearrange("p (c i) t -> p c t i", i=4),
-                in_=gw[n * SPAN // HALF][:, :, at : at + SPAN].rearrange("p t (c i) -> p c t i", i=4),
+                in_=gw[start // HALF][:, :, start % HALF : start % HALF + width].rearrange("p t (c i) -> p c t i", i=4),
             )
 
         def mix_rows(n):
-            gw_code = keep.tile([P, SPAN], U32, name="gw_code%d" % n, align_bytes=64)
-            gw_scale = keep.tile([P, SPAN], U8, name="gw_scale%d" % n, align_bytes=64)
+            start, width = spans[n]
+            gw_code = keep.tile([P, width], U32, name="gw_code%d" % n, align_bytes=64)
+            gw_scale = keep.tile([P, width], U8, name="gw_scale%d" % n, align_bytes=64)
             nc.vector.quantize_mx(
                 out=gw_code[:].bitcast(FP8X4), scales=gw_scale[:], in_=gw_bf[n][:].rearrange("p i t -> p (i t)")
             )
-            result = keep.tile([P, E // P, SPAN], F32, name="result%d" % n)
+            result = keep.tile([P, E // P, width], F32, name="result%d" % n)
             for m in range(E // P):
-                bank = psum.tile([P, SPAN], F32, name="bank", tag="bank")
+                bank = psum.tile([P, width], F32, name="bank", tag="bank")
                 nc.tensor.matmul_mx(
                     out=bank[:],
                     lhsT=mix_code[:, m * P : (m + 1) * P].bitcast(FP8X4),
@@ -253,9 +249,12 @@ def tile_attend_slotmix_one_mixed_kernel(
                     start=True,
                     stop=True,
                 )
-                leave_psum = nc.vector.tensor_copy if n == n_spans - 1 and m == 1 else nc.scalar.copy
+                leave_psum = nc.vector.tensor_copy if n >= 1 and m == 1 else nc.scalar.copy
                 leave_psum(out=result[:, m, :], in_=bank[:])
-            nc.sync.dma_start(out=out_view[:, :, n * SPAN : (n + 1) * SPAN], in_=result[:])
+                if n == 0:
+                    nc.sync.dma_start(out=out_view[:, m, start : start + width], in_=result[:, m, :])
+            if not (n == 0):
+                nc.sync.dma_start(out=out_view[:, :, start : start + width], in_=result[:])
 
         weave(0)
         for n in range(1, n_spans):

@@ -1,6 +1,7 @@
 from contextlib import ExitStack
 
 import concourse.mybir as mybir
+from concourse.masks import make_identity
 
 D, T, I, Q, E = 512, 1024, 512, 512, 256
 P = 128
@@ -12,6 +13,8 @@ HALF = I // 2
 LIST_COLS = I // 16
 W_FACTOR = 1.25
 KB = 1024
+GP = 128
+P1 = [128,128,256,256,256]
 
 F32 = mybir.dt.float32
 BF16 = mybir.dt.bfloat16
@@ -60,7 +63,7 @@ def tile_attend_slotmix_one_mixed_kernel(
         for u in range(2):
             nc.sync.dma_start(out=q_raw[u][:], in_=q_view[:, :, u * (Q // 2) : (u + 1) * (Q // 2)])
         key_scale = keep.tile([P, T], U8, name="key_scale", align_bytes=64)
-        load_scale_rows(nc.scalar, key_scale, keys_scales)
+        load_scale_rows(nc.sync, key_scale, keys_scales)
         key_code = keep.tile([P, 2 * T], U8, name="key_code", align_bytes=64)
         nc.sync.dma_start(out=key_code[:].bitcast(I32), in_=keys_words[0].bitcast(I32))
         nc.sync.dma_start(idx[:], offs)
@@ -98,15 +101,17 @@ def tile_attend_slotmix_one_mixed_kernel(
 
         w_at = {1: 0, 2: 7 * KB, 3: 15 * KB}
         c1_at = {0: 0, 1: 4 * KB, 2: 12 * KB}
-        scaled_at, a3_at = 16 * KB, 32 * KB
+        g1_at, turned_at, v0_at, identity_at = 16 * KB, 17 * KB, 21 * KB, 24 * KB
 
-        a = [keep.tile([P, T], F32, name="a%d" % t) for t in range(last)]
-        a.append(shared.tile([P, T], F32, name="a3", offset=a3_at))
+        identity = shared.tile([P, P], F32, name="identity", offset=identity_at)
+        make_identity(nc, identity[:])
+
+        a = [keep.tile([P, T], F32, name="a0"), keep.tile([P, T], F32, name="a1")]
+        a.extend(keep.tile([P, T], F32, name="a%d" % t) for t in (2, 3))
         m1 = [keep.tile([P, I], F32, name="m1_%d" % t) for t in range(PLACES)]
+        v = [shared.tile([P, I], F32, name="v0", offset=v0_at)]
+        v.extend(keep.tile([P, I], F32, name="v%d" % t) for t in range(1, PLACES))
         w, c1, score_banks = {}, {}, {}
-        v01 = keep.tile([P, 2 * I], F32, name="v01")
-        v = {0: v01[:, :I], 1: v01[:, I:]}
-        v.update({t: keep.tile([P, I], F32, name="v%d" % t)[:] for t in (2, 3)})
 
         def scores(t, width):
             score_banks[t] = []
@@ -122,10 +127,12 @@ def tile_attend_slotmix_one_mixed_kernel(
                     stop=True,
                 )
                 score_banks[t].append(bank)
-            for n in range(T // PIECE):
-                at = n * PIECE % width
+            start = 0
+            for n, piece in enumerate(P1 if t == 1 else [PIECE] * 4):
+                at = start % width
                 leave_psum = nc.vector.tensor_copy if t == 0 and n % 2 == 0 else nc.scalar.copy
-                leave_psum(out=a[t][:, n * PIECE : (n + 1) * PIECE], in_=score_banks[t][n * PIECE // width][:, at : at + PIECE])
+                leave_psum(out=a[t][:, start : start + piece], in_=score_banks[t][start // width][:, at : at + piece])
+                start = start + piece
 
         def look_up_w(t):
             w[t] = shared.tile([P, I], F32, name="w%d" % t, offset=w_at[t])
@@ -164,70 +171,81 @@ def tile_attend_slotmix_one_mixed_kernel(
 
         scores(last, BANK)
         look_up_w(last)
-        picked0_lo = shared.tile([P, HALF], F32, name="picked0_lo", offset=8 * KB)
-        g0_lo = keep.tile([P, HALF], F32, name="g0_lo")
-        nc.scalar.activation(picked0_lo[:], c1[0][:].indirect(half_list(idx4, 0)), COPY)
-        nc.gpsimd.tensor_tensor(g0_lo[:], picked0_lo[:], v[0][:, lo], ALU.add)
         look_up_v(last)
-        picked_late = shared.tile([P, HALF + I], F32, name="picked_late", offset=a3_at)
-        picked0_hi, picked1 = picked_late[:, :HALF], picked_late[:, HALF:]
-        nc.scalar.activation(picked0_hi, c1[0][:].indirect(half_list(idx4, 1)), COPY)
-        larger(last)
-        take_off(last - 1)
-        scatter(last)
+        picked = {t: keep.tile([P, I], F32, name="picked%d" % t) for t in (0, 1)}
 
-        scaled = shared.tile([P, PLACES * I + 2 * I + HALF + I], F32, name="scaled", offset=scaled_at)
-        gw = [
-            scaled[:, h * PLACES * HALF : (h + 1) * PLACES * HALF].rearrange("p (t i) -> p t i", t=PLACES)
-            for h in range(2)
-        ]
-        v_scaled = {t: scaled[:, (PLACES + t - 2) * I : (PLACES + t - 1) * I] for t in (2, 3)}
-        g_late = scaled[:, (PLACES + 2) * I :]
-        g0_hi, g1 = g_late[:, :HALF], g_late[:, HALF:]
+        def look_up_c1(t, h):
+            nc.scalar.activation(picked[t][:, halves[h]], c1[t][:].indirect(half_list(idx4, h)), COPY)
+
+        gw = keep.tile([P, PLACES, I], F32, name="gw")
+        v_scaled = {}
 
         def times_rowf(t, dest, source):
             nc.scalar.activation(dest, source, COPY, scale=row_factor[:, t : t + 1])
 
-        def scale_and_add(t, h, picked):
+        def scale_and_add(t, h):
             nc.vector.scalar_tensor_tensor(
-                gw[h][:, t, :], picked[:, halves[h]], row_factor[:, t : t + 1], v_scaled[t][:, halves[h]], ALU.mult, ALU.add
+                gw[:, t, halves[h]], picked[t][:, halves[h]], row_factor[:, t : t + 1], v_scaled[t][:, halves[h]], ALU.mult, ALU.add
             )
 
-        nc.scalar.activation(picked1, c1[1][:].indirect(idx4[:]), COPY)
-        nc.gpsimd.tensor_tensor(g_late, picked_late[:], v01[:, HALF:], ALU.add)
-        times_rowf(0, gw[0][:, 0, :], g0_lo[:])
-        for t in (2, 3):
-            times_rowf(t, v_scaled[t], v[t][:])
-        picked2 = keep.tile([P, I], F32, name="picked2")
-        nc.scalar.activation(picked2[:], c1[2][:].indirect(idx4[:]), COPY)
+        def add_on_tensor(t, start, width):
+            turned = psum.tile([P, width], F32, name="bank", tag="bank")
+            for n in range(width // P):
+                cols = slice(start + n * P, start + (n + 1) * P)
+                dest = turned[:, n * P : (n + 1) * P]
+                nc.tensor.matmul(dest, lhsT=picked[t][:, cols], rhs=identity[:], start=True, stop=False, is_transpose=True)
+                nc.tensor.matmul(dest, lhsT=v[t][:, cols], rhs=identity[:], start=False, stop=True, is_transpose=True)
+            g_turned = shared.tile([P, width], F32, name="g_turned%d" % t, offset=turned_at)
+            nc.scalar.copy(out=g_turned[:], in_=turned[:])
+            back = psum.tile([P, width], F32, name="bank", tag="bank")
+            for n in range(width // P):
+                nc.tensor.transpose(back[:, n * P : (n + 1) * P], g_turned[:, n * P : (n + 1) * P], identity[:])
+            times_rowf(t, gw[:, t, start : start + width], back[:])
 
-        c1[last] = keep.tile([P, T], F32, name="c1_3")
+        nc.scalar.activation(picked[0][:], c1[0][:].indirect(idx4[:]), COPY)
+        add_on_tensor(0, 0, I)
+        larger(last)
+        take_off(last - 1)
+        scatter(last)
+
+        v_scaled[2] = shared.tile([P, I], F32, name="v_scaled2", offset=v0_at - KB)
+        v_scaled[3] = shared.tile([P, I], F32, name="v_scaled3", offset=v0_at + KB)
+        nc.scalar.activation(picked[1][:], c1[1][:].indirect(idx4[:]), COPY)
+        g1 = shared.tile([P, I], F32, name="g1", offset=g1_at)
+        nc.gpsimd.tensor_tensor(g1[:], picked[1][:], v[1][:], ALU.add)
+        for t in (2, 3):
+            times_rowf(t, v_scaled[t][:], v[t][:])
+        picked[2] = shared.tile([P, I], F32, name="picked2", offset=turned_at + KB)
+        nc.scalar.activation(picked[2][:], c1[2][:].indirect(idx4[:]), COPY)
+
+
+        times_rowf(1, gw[:, 1, :], g1[:])
+
+        c1[last] = shared.tile([P, T], F32, name="c1_3", offset=identity_at)
         for n in range(T // BANK):
-            cols = slice(n * BANK, (n + 1) * BANK)
-            nc.vector.tensor_tensor(c1[last][:, cols], score_banks[last][n][:], f1[last % 2][:, cols], ALU.subtract)
-        picked3 = shared.tile([P, I], F32, name="picked3", offset=c1_at[2])
-        nc.scalar.activation(picked3[:, lo], c1[last][:].indirect(half_list(idx4, 0)), COPY)
-        nc.scalar.activation(picked3[:, hi], c1[last][:].indirect(half_list(idx4, 1)), COPY)
-        times_rowf(1, gw[0][:, 1, :], g1[:, lo])
-        times_rowf(1, gw[1][:, 1, :], g1[:, hi])
-        times_rowf(0, gw[1][:, 0, :], g0_hi)
-        scale_and_add(2, 0, picked2)
-        scale_and_add(2, 1, picked2)
-        scale_and_add(last, 0, picked3)
-        scale_and_add(last, 1, picked3)
+            width = BANK if n == 0 else BANK - GP
+            cols = slice(n * BANK, n * BANK + width)
+            nc.vector.tensor_tensor(c1[last][:, cols], score_banks[last][n][:, :width], f1[last % 2][:, cols], ALU.subtract)
+        nc.gpsimd.tensor_tensor(c1[last][:, T - GP :], a[last][:, T - GP :], f1[last % 2][:, T - GP :], ALU.subtract)
+        picked[last] = shared.tile([P, I], F32, name="picked3", offset=c1_at[2])
+        look_up_c1(last, 0)
+        look_up_c1(last, 1)
+        for t in (2, 3):
+            for h in range(2):
+                scale_and_add(t, h)
 
         out_view = out.rearrange("(m p) i -> p m i", p=P)
-        spans = [(0, 256), (256, 128), (384, 128)]
+        spans = [(0, 128), (128, 128), (256, 128), (384, 128)]
         n_spans = len(spans)
         gw_bf = {}
 
         def weave(n):
             start, width = spans[n]
-            gw_bf[n] = keep.tile([P, width, PLACES], BF16, name="gw_bf%d" % n, align_bytes=64)
-            round_and_weave = nc.scalar.copy if n == 1 else nc.vector.tensor_copy
+            gw_bf[n] = keep.tile([P, width, PLACES], BF16, name="gw_bf%d" % n, tag="gw_bf", bufs=3, align_bytes=64)
+            round_and_weave = nc.scalar.copy if n % 2 == 0 else nc.vector.tensor_copy
             round_and_weave(
                 out=gw_bf[n][:].rearrange("p (c i) t -> p c t i", i=4),
-                in_=gw[start // HALF][:, :, start % HALF : start % HALF + width].rearrange("p t (c i) -> p c t i", i=4),
+                in_=gw[:, :, start : start + width].rearrange("p t (c i) -> p c t i", i=4),
             )
 
         def mix_rows(n):
@@ -249,15 +267,12 @@ def tile_attend_slotmix_one_mixed_kernel(
                     start=True,
                     stop=True,
                 )
-                leave_psum = nc.vector.tensor_copy if n >= 1 and m == 1 else nc.scalar.copy
+                leave_psum = nc.vector.tensor_copy if n == 3 and m == 1 else nc.scalar.copy
                 leave_psum(out=result[:, m, :], in_=bank[:])
-                if n == 0:
-                    nc.sync.dma_start(out=out_view[:, m, start : start + width], in_=result[:, m, :])
-            if not (n == 0):
-                nc.sync.dma_start(out=out_view[:, :, start : start + width], in_=result[:])
+            nc.sync.dma_start(out=out_view[:, :, start : start + width], in_=result[:])
 
-        weave(0)
-        for n in range(1, n_spans):
+        for n in range(0, n_spans, 2):
             weave(n)
-            mix_rows(n - 1)
-        mix_rows(n_spans - 1)
+            weave(n + 1)
+            mix_rows(n)
+            mix_rows(n + 1)

from contextlib import ExitStack

import concourse.mybir as mybir
from concourse.masks import make_identity

D, T, I, Q, E = 512, 1024, 512, 512, 256
P = 128
PLACES = 4
BANK = 512
PIECE = 256
SPAN = 128
HALF = I // 2
LIST_COLS = I // 16
W_FACTOR = 1.25
KB = 1024
GP = 128
P1 = [128,128,256,256,256]

F32 = mybir.dt.float32
BF16 = mybir.dt.bfloat16
U32 = mybir.dt.uint32
I32 = mybir.dt.int32
U16 = mybir.dt.uint16
U8 = mybir.dt.uint8
FP8X4 = mybir.dt.float8_e4m3fn_x4
FP4X4 = mybir.dt.float4_e2m1fn_x4
ALU = mybir.AluOpType
COPY = mybir.ActivationFunctionType.Copy

FLOPS = 2 * D * Q * T + 2 * Q * E * I


def tile_attend_slotmix_one_mixed_kernel(
    tc, query, keys_words, keys_scales, rowf, mix_words, mix_scales, offs, offs2, offs3, offs4, out
):
    nc = tc.nc
    last = PLACES - 1
    halves = (slice(0, HALF), slice(HALF, I))
    lo, hi = halves
    with ExitStack() as ctx:
        lists = ctx.enter_context(tc.tile_pool(name="lists", bufs=1))
        keep = ctx.enter_context(tc.tile_pool(name="keep", bufs=1))
        shared = ctx.enter_context(tc.tile_pool(name="shared", bufs=1))
        psum = ctx.enter_context(tc.psum_pool(name="psum", bufs=8))

        idx = lists.tile([P, LIST_COLS], U16, name="idx")
        idx2 = lists.tile([P, LIST_COLS], U16, name="idx2")
        idx3 = lists.tile([P, LIST_COLS], U16, name="idx3")
        idx4 = lists.tile([P, LIST_COLS], U16, name="idx4")

        def half_list(list_tile, h):
            return list_tile[:, h * (LIST_COLS // 2) : (h + 1) * (LIST_COLS // 2)]

        def load_scale_rows(queue, plane, rows):
            for quad in range(4):
                queue.dma_start(
                    out=plane[32 * quad : 32 * quad + 4, :].bitcast(I32),
                    in_=rows[0, 4 * quad : 4 * quad + 4, :].bitcast(I32),
                )

        q_view = query.rearrange("(p j) q -> p j q", j=PLACES)
        q_raw = [keep.tile([P, PLACES, Q // 2], F32, name="q_raw%d" % u) for u in range(2)]
        for u in range(2):
            nc.sync.dma_start(out=q_raw[u][:], in_=q_view[:, :, u * (Q // 2) : (u + 1) * (Q // 2)])
        key_scale = keep.tile([P, T], U8, name="key_scale", align_bytes=64)
        load_scale_rows(nc.sync, key_scale, keys_scales)
        key_code = keep.tile([P, 2 * T], U8, name="key_code", align_bytes=64)
        nc.sync.dma_start(out=key_code[:].bitcast(I32), in_=keys_words[0].bitcast(I32))
        nc.sync.dma_start(idx[:], offs)
        nc.sync.dma_start(idx2[:], offs2)
        nc.sync.dma_start(idx3[:], offs3)
        nc.sync.dma_start(idx4[:], offs4)
        row_factor = keep.tile([P, PLACES], F32, name="row_factor")
        nc.sync.dma_start(out=row_factor[:], in_=rowf.rearrange("(p t) o -> p (t o)", t=PLACES))
        mix_code = keep.tile([P, E], U32, name="mix_code", align_bytes=64)
        nc.sync.dma_start(out=mix_code[:].bitcast(I32), in_=mix_words[0].rearrange("p e r -> p (e r)").bitcast(I32))
        mix_scale = keep.tile([P, E], U8, name="mix_scale", align_bytes=64)
        load_scale_rows(nc.sync, mix_scale, mix_scales)

        f1 = [keep.tile([P, T], F32, name="f1_%d" % b) for b in range(2)]
        for b in range(2):
            nc.vector.memset(f1[b][:], 0.0)

        q_first = keep.tile([P, P, PLACES], BF16, name="q_first", align_bytes=64)
        q_rest = keep.tile([P, last, P, PLACES], BF16, name="q_rest", align_bytes=64)
        for u in range(2):
            cols = slice(u * (P // 2), (u + 1) * (P // 2))
            dealt = q_raw[u][:].rearrange("p j (m t) -> p m j t", t=PLACES)
            nc.vector.tensor_copy(out=q_first[:, cols, :], in_=dealt[:, :, :, 0])
            cast_rest = nc.vector.tensor_copy if u == 0 else nc.scalar.copy
            cast_rest(out=q_rest[:, :, cols, :].rearrange("p t m j -> p m j t"), in_=dealt[:, :, :, 1:])

        q_code, q_scale = [], []
        for t in range(PLACES):
            q_code.append(keep.tile([P, P], U32, name="q_code%d" % t, align_bytes=64))
            q_scale.append(keep.tile([P, P], U8, name="q_scale%d" % t, align_bytes=64))
            rounded = q_first[:] if t == 0 else q_rest[:, t - 1]
            nc.vector.quantize_mx(
                out=q_code[t][:].bitcast(FP8X4), scales=q_scale[t][:], in_=rounded.rearrange("p m j -> p (m j)")
            )

        w_at = {1: 0, 2: 7 * KB, 3: 15 * KB}
        c1_at = {0: 0, 1: 4 * KB, 2: 12 * KB}
        g1_at, turned_at, v0_at, identity_at = 16 * KB, 17 * KB, 21 * KB, 24 * KB

        identity = shared.tile([P, P], F32, name="identity", offset=identity_at)
        make_identity(nc, identity[:])

        a = [keep.tile([P, T], F32, name="a0"), keep.tile([P, T], F32, name="a1")]
        a.extend(keep.tile([P, T], F32, name="a%d" % t) for t in (2, 3))
        m1 = [keep.tile([P, I], F32, name="m1_%d" % t) for t in range(PLACES)]
        v = [shared.tile([P, I], F32, name="v0", offset=v0_at)]
        v.extend(keep.tile([P, I], F32, name="v%d" % t) for t in range(1, PLACES))
        w, c1, score_banks = {}, {}, {}

        def scores(t, width):
            score_banks[t] = []
            for n in range(T // width):
                bank = psum.tile([P, width], F32, name="bank", tag="bank")
                nc.tensor.matmul_mx(
                    out=bank[:],
                    lhsT=q_code[t][:].bitcast(FP8X4),
                    lhsT_scale=q_scale[t][:],
                    rhs=key_code[:, 2 * width * n : 2 * width * (n + 1)].bitcast(FP4X4),
                    rhs_scale=key_scale[:, width * n : width * (n + 1)],
                    start=True,
                    stop=True,
                )
                score_banks[t].append(bank)
            start = 0
            for n, piece in enumerate(P1 if t == 1 else [PIECE] * 4):
                at = start % width
                leave_psum = nc.vector.tensor_copy if t == 0 and n % 2 == 0 else nc.scalar.copy
                leave_psum(out=a[t][:, start : start + piece], in_=score_banks[t][start // width][:, at : at + piece])
                start = start + piece

        def look_up_w(t):
            w[t] = shared.tile([P, I], F32, name="w%d" % t, offset=w_at[t])
            nc.scalar.activation(w[t][:], a[t][:].indirect(idx[:]), COPY, scale=W_FACTOR)

        def look_up_v(t):
            for h in range(2):
                nc.scalar.activation(v[t][:, halves[h]], w[t][:].indirect(half_list(idx2, h)), COPY)

        def larger(t):
            nc.vector.tensor_tensor(m1[t][:], w[t][:], v[t][:], ALU.max)

        def scatter(t):
            nc.vector.tensor_copy(f1[t % 2][:].indirect(idx3[:]), m1[t][:])

        def take_off(t):
            c1[t] = shared.tile([P, T], F32, name="c1_%d" % t, offset=c1_at[t])
            nc.gpsimd.tensor_tensor(c1[t][:], a[t][:], f1[t % 2][:], ALU.subtract)

        scores(0, PIECE)
        w[0] = keep.tile([P, I], F32, name="w0")
        nc.vector.tensor_scalar(w[0][:, lo], a[0][:].indirect(half_list(idx, 0)), W_FACTOR, 0.0, ALU.mult, ALU.add)
        nc.scalar.activation(w[0][:, hi], a[0][:].indirect(half_list(idx, 1)), COPY, scale=W_FACTOR)
        nc.vector.tensor_copy(v[0][:, lo], w[0][:].indirect(half_list(idx2, 0)))
        nc.scalar.activation(v[0][:, hi], w[0][:].indirect(half_list(idx2, 1)), COPY)
        larger(0)
        scatter(0)

        for t in (1, 2):
            scores(t, PIECE if t == 1 else BANK)
            look_up_w(t)
            look_up_v(t)
            larger(t)
            take_off(t - 1)
            scatter(t)

        scores(last, BANK)
        look_up_w(last)
        look_up_v(last)
        picked = {t: keep.tile([P, I], F32, name="picked%d" % t) for t in (0, 1)}

        def look_up_c1(t, h):
            nc.scalar.activation(picked[t][:, halves[h]], c1[t][:].indirect(half_list(idx4, h)), COPY)

        gw = keep.tile([P, PLACES, I], F32, name="gw")
        v_scaled = {}

        def times_rowf(t, dest, source):
            nc.scalar.activation(dest, source, COPY, scale=row_factor[:, t : t + 1])

        def scale_and_add(t, h):
            nc.vector.scalar_tensor_tensor(
                gw[:, t, halves[h]], picked[t][:, halves[h]], row_factor[:, t : t + 1], v_scaled[t][:, halves[h]], ALU.mult, ALU.add
            )

        def add_on_tensor(t, start, width):
            turned = psum.tile([P, width], F32, name="bank", tag="bank")
            for n in range(width // P):
                cols = slice(start + n * P, start + (n + 1) * P)
                dest = turned[:, n * P : (n + 1) * P]
                nc.tensor.matmul(dest, lhsT=picked[t][:, cols], rhs=identity[:], start=True, stop=False, is_transpose=True)
                nc.tensor.matmul(dest, lhsT=v[t][:, cols], rhs=identity[:], start=False, stop=True, is_transpose=True)
            g_turned = shared.tile([P, width], F32, name="g_turned%d" % t, offset=turned_at)
            nc.scalar.copy(out=g_turned[:], in_=turned[:])
            back = psum.tile([P, width], F32, name="bank", tag="bank")
            for n in range(width // P):
                nc.tensor.transpose(back[:, n * P : (n + 1) * P], g_turned[:, n * P : (n + 1) * P], identity[:])
            times_rowf(t, gw[:, t, start : start + width], back[:])

        nc.scalar.activation(picked[0][:], c1[0][:].indirect(idx4[:]), COPY)
        add_on_tensor(0, 0, I)
        larger(last)
        take_off(last - 1)
        scatter(last)

        v_scaled[2] = shared.tile([P, I], F32, name="v_scaled2", offset=v0_at - KB)
        v_scaled[3] = shared.tile([P, I], F32, name="v_scaled3", offset=v0_at + KB)
        nc.scalar.activation(picked[1][:], c1[1][:].indirect(idx4[:]), COPY)
        g1 = shared.tile([P, I], F32, name="g1", offset=g1_at)
        nc.gpsimd.tensor_tensor(g1[:], picked[1][:], v[1][:], ALU.add)
        for t in (2, 3):
            times_rowf(t, v_scaled[t][:], v[t][:])
        picked[2] = shared.tile([P, I], F32, name="picked2", offset=turned_at + KB)
        nc.scalar.activation(picked[2][:], c1[2][:].indirect(idx4[:]), COPY)


        times_rowf(1, gw[:, 1, :], g1[:])

        c1[last] = shared.tile([P, T], F32, name="c1_3", offset=identity_at)
        for n in range(T // BANK):
            width = BANK if n == 0 else BANK - GP
            cols = slice(n * BANK, n * BANK + width)
            nc.vector.tensor_tensor(c1[last][:, cols], score_banks[last][n][:, :width], f1[last % 2][:, cols], ALU.subtract)
        nc.gpsimd.tensor_tensor(c1[last][:, T - GP :], a[last][:, T - GP :], f1[last % 2][:, T - GP :], ALU.subtract)
        picked[last] = shared.tile([P, I], F32, name="picked3", offset=c1_at[2])
        look_up_c1(last, 0)
        look_up_c1(last, 1)
        for t in (2, 3):
            for h in range(2):
                scale_and_add(t, h)

        out_view = out.rearrange("(m p) i -> p m i", p=P)
        spans = [(0, 128), (128, 128), (256, 128), (384, 128)]
        n_spans = len(spans)
        gw_bf = {}

        def weave(n):
            start, width = spans[n]
            gw_bf[n] = keep.tile([P, width, PLACES], BF16, name="gw_bf%d" % n, tag="gw_bf", bufs=3, align_bytes=64)
            round_and_weave = nc.scalar.copy if n % 2 == 0 else nc.vector.tensor_copy
            round_and_weave(
                out=gw_bf[n][:].rearrange("p (c i) t -> p c t i", i=4),
                in_=gw[:, :, start : start + width].rearrange("p t (c i) -> p c t i", i=4),
            )

        def mix_rows(n):
            start, width = spans[n]
            gw_code = keep.tile([P, width], U32, name="gw_code%d" % n, align_bytes=64)
            gw_scale = keep.tile([P, width], U8, name="gw_scale%d" % n, align_bytes=64)
            nc.vector.quantize_mx(
                out=gw_code[:].bitcast(FP8X4), scales=gw_scale[:], in_=gw_bf[n][:].rearrange("p i t -> p (i t)")
            )
            result = keep.tile([P, E // P, width], F32, name="result%d" % n)
            for m in range(E // P):
                bank = psum.tile([P, width], F32, name="bank", tag="bank")
                nc.tensor.matmul_mx(
                    out=bank[:],
                    lhsT=mix_code[:, m * P : (m + 1) * P].bitcast(FP8X4),
                    lhsT_scale=mix_scale[:, m * P : (m + 1) * P],
                    rhs=gw_code[:].bitcast(FP8X4),
                    rhs_scale=gw_scale[:],
                    start=True,
                    stop=True,
                )
                leave_psum = nc.vector.tensor_copy if n == 3 and m == 1 else nc.scalar.copy
                leave_psum(out=result[:, m, :], in_=bank[:])
            nc.sync.dma_start(out=out_view[:, :, start : start + width], in_=result[:])

        for n in range(0, n_spans, 2):
            weave(n)
            weave(n + 1)
            mix_rows(n)
            mix_rows(n + 1)
